import numpy as np, ml_dtypes
CORES = [16,17,18,19,32,33,34,35]
N = 8
BF = ml_dtypes.bfloat16
def gentries(a):
    return np.ascontiguousarray(a.reshape(8, 16, -1).transpose(0, 2, 1)).reshape(8, -1)
def gtable(e):
    e = np.asarray(e); return np.ascontiguousarray(e.reshape(8, -1, 16).transpose(0, 2, 1)).reshape(128, -1).astype(np.int32)
Q, A, S, RO, B = 512, 256, 2, 4, 2048
W, H = N * Q, A // 4
def some(rng, shape, n):
    u = rng.random(shape); u = np.where(rng.random(shape) < 0.5, u, u * u)
    return np.minimum((n * u).astype(np.int64), n - 1)
def parts(rng):
    F = (rng.integers(0, 256, (8, 16, W)) * np.sqrt(rng.random((8, 1, W)))).astype(np.int64)
    NB = np.zeros((8, 16, W), np.int64); HO = np.zeros((N, 8, A), np.int64)
    for g in range(8):
        o = rng.permutation(W); NB[g] = o[some(rng, (16, W), W)]; HO[:, g] = o[some(rng, (N, A), W)]
    return F, NB, HO
def plant(rng):
    F, NB, HO = parts(rng); own = np.zeros((N, 8, H, S + 3), np.int64); k = N * H * (S + 3)
    for g in range(8):
        o = rng.permutation(W); mine, rest = o[:k], o[k:]
        own[:, g] = mine.reshape(N, H, S + 3)
        NB[g] = rest[some(rng, (16, W), W - k)]; HO[:, g] = rest[some(rng, (N, A), W - k)]
        for r in range(N): HO[r, g, rng.permutation(A)[:H]] = own[r, g, :, 0]
        NB[g][:, mine] = mine; F[g][:, mine] = 0
    return F, NB, HO, own
def lead(rng, NB, g, t, *cs):
    z = np.argsort(rng.random((16, len(t))), axis=0)
    for i, c in enumerate(cs):
        NB[g, z[2 * i], t] = c; NB[g, z[2 * i + 1], t] = c
def climb(rng, F, NB, g, e):
    n = len(e); m = np.zeros((16, n), np.int64)
    for k in range(S + 1):
        a = rng.integers(0, 40, (16, n)) * (rng.random((16, n)) < 0.2 * rng.random((1, n))); a[rng.integers(0, 16, n), np.arange(n)] += 1
        m = m + a; F[g][:, e[:, 1 + k]] = m; lead(rng, NB, g, e[:, k], e[:, 1 + k])
def pack(F, NB, HO):
    return {"feat": np.stack([F[:, :, r * Q:(r + 1) * Q].reshape(128, Q) for r in range(N)]).astype(np.float32).astype(BF),
            "nb": np.stack([NB[:, :, r * Q:(r + 1) * Q].reshape(128, Q) for r in range(N)]).astype(np.int32),
            "home": np.stack([gtable(a) for a in HO])}
def setup_inputs(rng):
    F, NB, HO = parts(rng)
    return pack(F, NB, HO)
def setup_inputs_cut(rng):
    F, NB, HO, own = plant(rng); j = np.arange(H); odd = j % 2 == 1
    for g in range(8):
        for r in range(N):
            e = own[r, g]
            if r % 2 == 0:
                u = e[:, 1]; F[g][8:, u] = 255; lead(rng, NB, g, e[:, 0], u)
                lead(rng, NB, g, u, own[np.where(j < H // 2, (r + 1) % N, (r - 1) % N), g, j, 1])
            else:
                t = [e[:, 1 + k] for k in range(S + 1)]; alt = e[:, S + 2]
                m = np.zeros((16, H), np.int64); m[:8] = rng.integers(100, 181, (8, H)); F[g][:, t[0]] = m
                b = np.zeros((16, H), np.int64); b[8:] = rng.integers(1, 91, (8, H))
                for k in range(1, S + 1):
                    y = np.where(m > 0, m + rng.integers(1, 10, (16, H)), 0)
                    if k == 1: y = np.where(odd, b, y)
                    F[g][:, t[k]] = y; m = np.maximum(m, y); lead(rng, NB, g, t[k - 1], t[k])
                F[g][:8, alt] = rng.integers(1, 50, (8, H)); lead(rng, NB, g, alt, t[1])
                lead(rng, NB, g, e[:, 0], t[0], np.where(odd, t[1], alt))
    return pack(F, NB, HO)
def setup_inputs_full(rng):
    F, NB, HO = parts(rng); rf = int(rng.integers(0, N - 1)); n = A * (2 * S + 2); w = 16 // (2 * S - 1)
    for g in range(8):
        o = rng.permutation(W); mine, rest = o[:n], o[n:]; e = mine.reshape(A, 2 * S + 2)
        NB[g] = rest[some(rng, (16, W), W - n)]; HO[:, g] = rest[some(rng, (N, A), W - n)]
        NB[g][:, mine] = mine; F[g][:, mine] = 0; HO[rf, g] = e[:, 0]
        if g % 2 == 0: climb(rng, F, NB, g, e)
        else:
            rn = N - 1 if rf == 0 and g > 4 else rf + 1
            k = np.arange(A) % S if g % 4 == 1 else np.full(A, S - 1)
            for i in range(2 * S - 1):
                F[g][w * i:w * i + w, e[:, 1 + i]] = rng.integers(1, 256, (w, A)); lead(rng, NB, g, e[:, i], e[:, 1 + i])
            want = e[np.arange(A), 1 + k]; x = e[:, 2 * S]; HO[rn, g] = e[:, 2 * S + 1]
            if g != 7: F[g][15, x] = 1
            lead(rng, NB, g, x, want); lead(rng, NB, g, e[:, 2 * S + 1], want, x)
    return pack(F, NB, HO)
def setup_inputs_same(rng):
    F, NB, HO = parts(rng)
    for g in range(8):
        if g % 2 == 0:
            kinds = rng.integers(0, 256, (16, 6)); kinds[:, 0] = 0; F[g] = kinds[:, rng.integers(0, 6, W)]
        if g < 2: HO[:, g] = rng.permutation(W)[:24][rng.integers(0, 24, (N, A))]
        if g % 4 == 3: NB[g, 8:] = NB[g, :8]
        if g in (4, 5):
            h = int(rng.integers(0, W)); t = int(rng.integers(0, N)) * Q + rng.permutation(Q)[:5]; t = t[t != h][:1 if g == 4 else 4]
            HO[:, g] = h; NB[g][:, h] = t[np.arange(16) % len(t)]; F[g][:, t] = rng.integers(1, 256, (16, len(t)))
    return pack(F, NB, HO)
def setup_inputs_ends(rng):
    F, NB, HO = parts(rng)
    F = 255 * (rng.random((8, 16, W)) < 0.6 * rng.random((8, 1, W))).astype(np.int64); F[:, :, 0] = 255; F[:, :, W - 1] = 255
    ends = np.concatenate([np.arange(N) * Q, np.arange(N) * Q + Q - 1])
    for g in range(8):
        if g % 2 == 0:
            NB[g] = np.where(rng.random((16, W)) < 0.3, rng.choice(ends, (16, W)), NB[g])
            HO[:, g, ::3] = rng.choice(ends, HO[:, g, ::3].shape)
        if g % 4 == 1:
            m = np.nonzero(rng.random(W) < 0.3)[0]; NB[g][:, m] = m
        if g % 4 == 3:
            q = int(rng.integers(0, N)); NB[g] = q * Q + NB[g] % Q; HO[:, g] = q * Q + HO[:, g] % Q
    return pack(F, NB, HO)
def setup_inputs_spread(rng):
    F, NB, HO = parts(rng)
    F = (rng.random((8, 16, W)) * np.exp2(rng.integers(0, 9, (8, 1, W))) * (rng.random((8, 1, W)) > 0.0625)).astype(np.int64)
    for g in range(8):
        o = rng.permutation(W)
        NB[g] = o[np.minimum((W * rng.random((16, W)) ** 4).astype(np.int64), W - 1)]; HO[:, g] = o[np.minimum((W * rng.random((N, A)) ** 3).astype(np.int64), W - 1)]
    return pack(F, NB, HO)
def check_inputs(d):
    bad = []; v = np.asarray(d["feat"]).astype(np.float32)
    if not (np.min(v) >= 0 and np.max(v) <= 255 and np.all(v == np.floor(v))): bad.append("feat: whole numbers from 0 to 255")
    for k in ("nb", "home"):
        if np.min(d[k]) < 0 or np.max(d[k]) > W - 1: bad.append("range of " + k)
    return bad
def reference(feat, nb, home):
    F = np.concatenate([a.astype(np.float32).astype(np.int64).reshape(8, 16, Q) for a in feat], axis=2)
    C = np.concatenate([a.astype(np.int64).reshape(8, 16, Q) for a in nb], axis=2)
    F = np.ascontiguousarray(F.transpose(0, 2, 1)); C = np.ascontiguousarray(C.transpose(0, 2, 1))
    h = np.stack([gentries(a) for a in home]).astype(np.int64)
    ri = np.arange(N)[:, None, None]; gi = np.arange(8)[None, :, None]; ids = np.arange(N * A).reshape(N, 1, A, 1)
    bt = np.zeros((N, 8, S, A), np.int64); bk = np.zeros((N, 8, S, A), np.int64); cnt = np.zeros((N, 8, A), np.int64)
    T = np.zeros((N, 8, W), np.int64)
    for rnd in range(RO):
        V = np.maximum(T, np.maximum(np.roll(T, 1, axis=0), np.roll(T, -1, axis=0)))
        still = np.ones((N, 8, A), bool); n = np.zeros((N, 8, A), np.int64); M = np.zeros((N, 8, A, 16), np.int64); last = h
        for k in range(S):
            b = bt[:, :, k]
            still = still & (k < cnt) & (V[ri, gi, b] == bk[:, :, k])
            M = np.where(still[..., None], np.maximum(M, F[gi, b]), M); last = np.where(still, b, last); n = n + still
        c = C[gi, last]
        gain = np.add.reduce(np.maximum(F[gi[..., None], c] - M[:, :, :, None, :], 0), axis=-1)
        key = B * gain + (B - 1) - ids
        ok = (n < S)[..., None] & (gain > 0) & (key > V[ri[..., None], gi[..., None], c])
        p = np.argmax(np.where(ok, gain, 0), axis=-1)[..., None]
        ct = np.take_along_axis(c, p, -1)[..., 0]; kt = np.take_along_axis(key, p, -1)[..., 0]; bid = np.any(ok, axis=-1)
        best = np.zeros((N, 8, W), np.int64); np.maximum.at(best, (ri, gi, ct), np.where(bid, kt, 0))
        win = bid & (best[ri, gi, ct] == kt)
        T = np.zeros((N, 8, W), np.int64)
        for k in range(S):
            w = np.nonzero(k < n); T[w[0], w[1], bt[:, :, k][w]] = bk[:, :, k][w]
        w = np.nonzero(win); T[w[0], w[1], ct[w]] = kt[w]
        bt[w[0], w[1], n[w], w[2]] = ct[w]; bk[w[0], w[1], n[w], w[2]] = kt[w]; cnt = n + win
    yb = np.where(np.arange(S)[None, None, :, None] < cnt[:, :, None, :], bt, -1)
    return {"yb": yb.reshape(N, 8, S * A).astype(np.float32), "yt": T.astype(np.float32)}

import numpy as np
from concourse.bass import DstId, RemoteDMATransfer
from concourse.mybir import AluOpType as ALU, AxisListType, ActivationFunctionType as AF

N = 8
W = 4096
RO = 4
BIG = float(2 ** 19)

SCRATCH = {
    "nbs": ("sbuf", [128, 512], "int32"), "hs": ("sbuf", [128, 16], "int32"), "sb16": ("sbuf", [128, 528], "uint16"),
    "dF": ("dram", [8, 128, 64], "bfloat16"), "d16": ("dram", [8, 128, 66], "uint16"),
    "LF": ("dram", [8, 128, 64], "bfloat16"), "LN": ("dram", [8, 128, 66], "uint16"),
    "Fb0": ("sbuf", [128, 256], "bfloat16"), "Fb1": ("sbuf", [128, 256], "bfloat16"),
    "Nb0": ("sbuf", [128, 264], "uint16"), "Nb1": ("sbuf", [128, 264], "uint16"),
    "HL": ("sbuf", [128, 16], "uint16"),
    "NBf": ("sbuf", [128, 512], "float32"), "NBh": ("sbuf", [128, 512], "float16"), "Yt": ("sbuf", [128, 512], "float32"),
    "OT": ("sbuf", [128, 512], "uint16"), "Mt": ("sbuf", [128, 512], "bfloat16"),
    "Gm": ("sbuf", [128, 8192], "bfloat16"), "G1s": ("sbuf", [128, 528], "float32"), "Gx": ("sbuf", [128, 1024], "float16"),
    "Gf": ("sbuf", [128, 512], "bfloat16"), "Ib": ("sbuf", [128, 256], "bfloat16"),
    "Fw": ("sbuf", [128, W], "bfloat16"), "NBw": ("sbuf", [128, W + 256], "float32"), "Gw": ("sbuf", [128, W + 256], "float32"),
    "Tw": ("sbuf", [128, W + 512], "float32"), "Vw": ("sbuf", [128, W + 256], "float32"), "Cw": ("sbuf", [128, W], "bfloat16"),
    "GV": ("sbuf", [128, W], "float32"), "GB": ("sbuf", [128, W], "bfloat16"), "CG": ("sbuf", [128, 1536], "float32"),
    "ki": ("sbuf", [128, 16], "int32"), "kf": ("sbuf", [128, 24], "float32"), "cf": ("sbuf", [128, 160], "float32"),
    "co": ("sbuf", [128, 160], "uint16"), "ct": ("sbuf", [128, 512], "float32"), "ones": ("sbuf", [128, 256], "bfloat16"),
    "SELb": ("sbuf", [128, 1024], "bfloat16"), "SELh": ("sbuf", [128, 1024], "float16"), "SELg": ("sbuf", [128, 512], "float16"),
    "U": ("sbuf", [128, 144], "bfloat16"), "BDn": ("sbuf", [128, 128], "bfloat16"), "CI": ("sbuf", [128, 256], "float32"),
    "NI": ("sbuf", [128, 128], "float32"), "MQ": ("sbuf", [128, 256], "float32"), "RU": ("sbuf", [128, 8], "float32"),
    "RU32": ("sbuf", [128, 8], "bfloat16"), "SV": ("sbuf", [128, 768], "float32"),
    "SVb": ("sbuf", [128, 768], "float32"), "DL": ("sbuf", [128, 48], "float32"),
    "dum": ("sbuf", [128, 16], "float32"), "idp": ("sbuf", [128, 16], "float32"), "ida": ("sbuf", [128, 16], "float32"),
    "P15": ("sbuf", [128, 128], "float32"), "RST": ("sbuf", [128, 128], "float32"),
    "sgn": ("sbuf", [128, 16], "float32"), "acol": ("sbuf", [128, 16], "float32"), "zer": ("sbuf", [128, 512], "float32"),
    "off": ("sbuf", [128, 256], "uint16"), "crow": ("sbuf", [128, 256], "float32"), "grow": ("sbuf", [128, 256], "float32"),
    "m0": ("sbuf", [128, 256], "float32"), "m1": ("sbuf", [128, 256], "float32"), "m2": ("sbuf", [128, 256], "float32"),
    "m3": ("sbuf", [128, 256], "float32"), "m4": ("sbuf", [128, 256], "float32"), "m5": ("sbuf", [128, 256], "float32"),
    "sc": ("sbuf", [128, 256], "float32"),
    "sc1": ("sbuf", [128, 256], "float32"), "sc2": ("sbuf", [128, 256], "float32"), "KEY": ("sbuf", [128, 256], "float32"),
    "EX": ("sbuf", [128, 768], "float32"), "EX2": ("sbuf", [128, 512], "float32"), "KX": ("sbuf", [128, 256], "float32"),
    "Pv": ("sbuf", [128, 256], "float32"), "Bt": ("sbuf", [128, 256], "bfloat16"), "At": ("sbuf", [128, 512], "bfloat16"),
    "junk": ("sbuf", [128, 4096], "bfloat16"), "lu": ("sbuf", [128, 16], "uint16"), "bu": ("sbuf", [128, 16], "uint16"),
    "wu": ("sbuf", [128, 16], "uint16"), "du": ("sbuf", [128, 32], "uint16"), "CL": ("sbuf", [128, 96], "uint16"),
    "BL": ("sbuf", [128, 32], "float32"), "st": ("sbuf", [128, 1280], "float32"),
    "dT": ("dram", [8, 128, 32], "float32"), "LT": ("dram", [8, 128, 32], "float32"),
    "msg": ("sbuf", [128, 64], "float32"), "rcv": ("sbuf", [128, 64], "float32"), "ybs": ("sbuf", [8, 512], "float32"),
}
for _b in range(8):
    SCRATCH["ps%d" % _b] = ("psum", [128, 512], "float32")

SEMAPHORES = ["cv", "ca", "ct", "cg", "sent", "fA", "fB", "nA", "nB", "tab", "fin"] + ["d%d" % i for i in range(24)]

ST = ["f1b", "f1c", "f1a", "f0a", "f0b", "f0c", "k1", "k0", "k0b", "k1b", "S1d", "S0d", "K0", "K1", "S0a", "K0a", "K1a",
      "n0", "n0b", "n1", "csd", "kp", "kpb", "e1", "e2", "e3", "a1", "a0", "DR1", "DR0",
      "x1", "x2", "x3", "XL", "cb", "cs", "csa", "csb", "mm", "g32", "key", "bid", "nthr", "thv", "R", "w", "XW", "Lf", "Lm",
      "a2", "a3", "c1", "c5", "y1", "y2",
      "D0", "D1", "D2", "D3", "B0", "B1", "B2", "B3", "Dm0", "Dm1", "Dm2", "Dm3", "Bm0", "Bm1", "Bm2", "Bm3",
      "mt0", "mt1", "mt2", "mt3"]

CYC, PEC, FIX, WAKE = 1.04e-3, 0.52e-3, 0.05, 0.08
ARRIVE = {"fA": 5.0, "fB": 9.0, "nA": 3.3, "nB": 10.3, "tab": 7.0, "fin": 3.5}
WIDE = {"float32": 4, "int32": 4, "bfloat16": 2, "float16": 2, "uint16": 2}
D1, D2 = 11.0, 34.0
TRIES, SEED, TEMP = 2500, 1, 0.3
R1V = ()
RVV = (0, 1, 4)
NV = (0, 4, 4, 4)
GS = (10, 11, 12, 13, 14, 15)


def rank_program(g, core, T, topo):
    me = T.rank_of(core)
    if me is None:
        return
    cores = list(T.cores)
    near = [r for r in range(N) if topo.chip(cores[r]) == topo.chip(core)]
    far = [r for r in range(N) if r not in near]
    assert len(near) == 4 and near == list(range(near[0], near[0] + 4)) and far == list(range(far[0], far[0] + 4))
    RB = [near[0], far[0]]
    Q = {"v": g.vector, "a": g.scalar, "t": g.tensor, "g": g, "s": g.sync}
    ops = []
    mode = [None, None]
    ALLP = (1 << 128) - 1

    def v(name, a=None, b=None, s=None, p0=0, p1=None, ps=None):
        t = T[name]
        p1 = t.shape[0] if p1 is None else p1
        a = 0 if a is None else a
        b = t.shape[1] if b is None else b
        if name[:2] == "ps":
            reg = (name, 1, ALLP)
        else:
            cols = (1 << b) - (1 << a) if s is None else sum(1 << c for c in range(a, b, s))
            reg = (name, cols, sum(1 << p for p in range(p0, p1, ps or 1)))
        return (t[slice(p0, p1, ps), slice(a, b, s)], [reg], len(range(a, b, s or 1)), False)

    def d(name, ap_, a=0, b=8):
        return (ap_, [(name, (1 << b) - (1 << a), ALLP)], 0, False)

    def s_(name, n=1):
        i = ST.index(name) * 16
        return v("st", i, i + 16 * n)

    def sx(name, a, b, s=None):
        i = ST.index(name) * 16
        return v("st", i + a, i + b, s)

    def ind(win, off):
        return (win[0].indirect(off[0]), win[1] + off[1], 16 * off[2], True)

    def add(eng, fn, outs, ins, cost, dsem=None, waits=(), feeds=()):
        wr = []
        rd = []
        for o in outs:
            wr += o[1][:1]
            rd += o[1][1:]
        for i in ins:
            if isinstance(i, tuple):
                rd += i[1]
        ops.append({"e": eng, "fn": fn, "w": wr, "r": rd, "dsem": dsem, "waits": list(waits), "c": cost, "feeds": feeds,
                    "due": mode[0], "chain": mode[1]})

    def ap(x):
        return x[0] if isinstance(x, tuple) else x

    def cost(o, ins, two=False):
        sc_ = lambda x: SCRATCH[x[1][0][0]]
        if o[3]:
            c = 3.8
        elif any(i[3] for i in ins):
            c = 1.5
        elif two:
            c = 2.0 if all(sc_(i)[0] == "sbuf" for i in ins) else 1.0
        else:
            c = 0.5 if all(WIDE[sc_(i)[2]] == 2 for i in ins + [o]) else 1.0
        return FIX + max(64, c * max([o[2]] + [i[2] for i in ins])) * CYC

    def cp(o, i, waits=()):
        add("v", lambda q: q.tensor_copy(o[0], i[0]), [o], [i], cost(o, [i]), waits=waits)

    def tt(o, a, b, op):
        add("v", lambda q: q.tensor_tensor(o[0], a[0], b[0], op), [o], [a, b], cost(o, [a, b], True))

    def ts(o, a, s1, op0, s2=None, op1=None):
        if op1 is None:
            add("v", lambda q: q.tensor_scalar(o[0], a[0], ap(s1), None, op0), [o], [a, s1], cost(o, [a]))
        else:
            add("v", lambda q: q.tensor_scalar(o[0], a[0], ap(s1), ap(s2), op0, op1), [o], [a, s1, s2], cost(o, [a]))

    def mset(o, c):
        add("v", lambda q: q.memset(o[0], c), [o], [], cost(o, []))

    def scan(o, a, b, op0, op1):
        add("v", lambda q: q.tensor_tensor_scan(o[0], a[0], b[0], 0.0, op0, op1), [o], [a, b], cost(o, [a]))

    def act(o, i, func=AF.Identity, bias=0.0, scale=1.0, acc=None):
        c = FIX + 0.015 + max(64, (3.8 if o[3] else 1.5 if i[3] else 1.0) * max(o[2], i[2])) * CYC
        if func in (AF.Copy, AF.Tanh, AF.Sign):
            add("a", lambda q: q.activation(o[0], i[0], func), [o], [i], c)
        elif acc is None:
            add("a", lambda q: q.activation(o[0], i[0], func, bias=ap(bias), scale=ap(scale)), [o], [i, bias, scale], c)
        else:
            add("a", lambda q: q.activation(o[0], i[0], func, bias=ap(bias), scale=ap(scale), accum_out=acc[0]),
                [o, acc], [i, bias, scale], c + 0.02)

    def mm(o, l, r, start=True, stop=True, waits=()):
        c = max(min(64, l[2]), r[2]) * PEC * (4 if SCRATCH[l[1][0][0]][2] == "float32" else 1) + 0.01
        add("t", lambda q: q.matmul(o[0], l[0], r[0], start, stop), [o], [l, r], c, waits=waits)

    def dma(eng, o, i, sem, waits=(), c=2.3):
        add(eng, lambda q: q.dma_start(o[0], i[0]), [o], [i], c, dsem=sem, waits=waits)

    def iota(o, pat, base, cm):
        c = 0.13 + 2 * o[2] * CYC
        if o[1][0][0] == "ki":
            add("g", lambda q: q.iota(o[0], pat, base, cm), [o], [], c)
        else:
            add("g", lambda q: q.iota(o[0], pat, base, cm, allow_small_or_imprecise_dtypes=True), [o], [], c)

    def asel(o, i, pat, base, cm, op=ALU.is_equal, fill=0.0):
        add("g", lambda q: q.affine_select(o[0], i[0], pat, op, fill, base, cm), [o], [i], 0.17 + 2 * o[2] * CYC)

    kf = lambda j: v("kf", j, j + 1)
    ac = lambda j: v("acol", j, j + 1)
    co = lambda a, b: v("co", a, b)
    EXP, E15, PERM, MA, GEXP, MW, MP, RX = 0, 32, 48, 64, 96, 128, 132, 136

    def evac(k, o, i, scale=1.0, col=None):
        if k % 2 == 0:
            if col is None:
                cp(o, i)
            else:
                ts(o, i, scale, ALU.mult, col, ALU.add)
        elif col is None:
            act(o, i, AF.Copy)
        else:
            act(o, i, AF.Identity, col, scale)

    sent = [0]

    def send(src, dst, sem_of, reads):
        eo = topo.engines(core, cores[far[0]])
        ei = [e for e in topo.engines(core, cores[[r for r in near if r != me][0]]) if e not in eo]
        trs = []
        for lst, eng in ((far, eo), ([r for r in near if r != me], ei)):
            for i, r in enumerate(lst):
                rid, pid, _ = topo.addr(cores[r])
                mask = (1 << eng[2 * i]) | (1 << eng[2 * i + 1])
                trs.append(RemoteDMATransfer(dst_ids=[DstId(rid=rid, pnc=pid)], dma_engine_mask=mask,
                                             remote_sem=T.sem[sem_of(r)], src=src(r), dst=dst))
        sent[0] += 14
        add("g", lambda q: q.remote_dma_fused(trs, local_sem=T.sem.sent), [d("wire", None)], reads, 0.5, dsem="remote",
            feeds=set(sem_of(r) for r in range(N) if r != me))

    nil = lambda x: (x, [], 0, False)
    dma("s", v("nbs"), nil(T.nb[:, :]), "d0", c=3.0)
    dma("a", d("dF", T.dF[:]), nil(T.feat[:, :]), "d1")
    dma("a", v("hs"), nil(T.home[:, :]), "d2")
    dma("s", d("LF", T.LF[me], me, me + 1), nil(T.feat[16 * me:16 * me + 16, :]), "d3")
    send(lambda r: T.dF[r], T.LF[me], lambda r: "fA" if r in near else "fB", [d("dF", None)])
    cp(v("sb16", 0, 256), v("nbs", 0, 256))
    cp(v("sb16", 264, 520), v("nbs", 256, 512))
    cp(v("sb16", 256, 264), v("hs", 0, 8))
    cp(v("sb16", 520, 528), v("hs", 8, 16))
    dma("s", d("d16", T.d16[:]), v("sb16"), "d4")
    dma("a", d("LN", T.LN[me], me, me + 1), v("sb16", p0=16 * me, p1=16 * me + 16), "d5")
    send(lambda r: T.d16[r], T.LN[me], lambda r: "nA" if r in near else "nB", [d("d16", None)])

    mode[0] = 9.0
    mset(v("zer"), 0.0)
    iota(v("ki", 0, 1), [[0, 1]], 0, 1)
    iota(v("ct", 0, 144), [[1, 144]], -15, 0)
    iota(v("ct", 144, 272), [[16, 8], [0, 16]], 0, 0)
    iota(v("MQ"), [[0, 16], [1, 16]], 0, 0)
    mset(v("ones"), 1.0)
    for r4 in range(4):
        asel(v("SELb", 256 * r4, 256 * r4 + 256), v("ones"), [[-1, 2], [0, 8], [-2, 16]], -32 * r4, 1)
        cp(v("SELh", 256 * r4, 256 * r4 + 256), v("SELb", 256 * r4, 256 * r4 + 256))
    for j, (o0, s0, o1, s1) in enumerate([(ALU.bitwise_and, 112, None, None), (ALU.bitwise_and, 15, None, None),
                                          (ALU.logical_shift_right, 5, None, None),
                                          (ALU.logical_shift_right, 4, ALU.bitwise_and, 1), (ALU.bitwise_and, 7, None, None),
                                          (ALU.logical_shift_right, 3, ALU.bitwise_and, 1), (ALU.bitwise_and, 31, None, None),
                                          (ALU.bitwise_and, 1, None, None)]):
        ts(v("ki", j + 1, j + 2), v("ki", 0, 1), s0, o0, s1, o1)
    cp(v("kf", 0, 9), v("ki", 0, 9))
    iota(v("cf", EXP, EXP + 32), [[1, 32]], 0, 0)
    iota(v("cf", E15, E15 + 16), [[16, 16]], 15, 0)
    iota(v("cf", PERM, PERM + 16), [[2, 16]], 0, 0)
    for b in range(2):
        iota(v("cf", MA + 16 * b, MA + 16 * b + 16), [[256, 2], [32, 8]], RB[b] * 512, 0)
    iota(v("cf", GEXP, GEXP + 32), [[16, 16], [0, 2]], -256, 0)
    iota(v("ct", 272, 304), [[0, 16], [1, 2]], 0, 0)
    iota(v("cf", MW, MW + 8), [[0, 2], [2, 4]], 0, 0)
    iota(v("cf", RX, RX + 16), [[1, 2], [8, 8]], 0, 0)
    ts(kf(10), kf(5), 32.0, ALU.mult, kf(6), ALU.add)
    ts(kf(11), kf(3), 512.0, ALU.mult, kf(7), ALU.add)
    ts(kf(12), kf(8), 8.0, ALU.mult, kf(6), ALU.add)
    ts(kf(13), kf(5), 8.0, ALU.mult, kf(6), ALU.add)
    ts(v("cf", PERM, PERM + 16), v("cf", PERM, PERM + 16), kf(10), ALU.add)
    ts(v("cf", MA, MA + 32), v("cf", MA, MA + 32), kf(11), ALU.add)
    ts(v("cf", MW, MW + 4), v("cf", MW, MW + 4), kf(12), ALU.add)
    ts(v("cf", MP, MP + 4), v("cf", MP, MP + 4), kf(13), ALU.add)
    ts(v("cf", GEXP, GEXP + 32), v("cf", GEXP, GEXP + 32), kf(2), ALU.add)
    ts(v("ct", 272, 304), v("ct", 272, 304), kf(4), ALU.is_equal)
    tt(v("cf", GEXP, GEXP + 32), v("cf", GEXP, GEXP + 32), v("ct", 272, 304), ALU.mult)
    ts(v("cf", GEXP, GEXP + 32), v("cf", GEXP, GEXP + 32), 256.0, ALU.add)
    cp(v("co", 0, 152), v("cf", 0, 152))
    mset(ac(4), 2048.0)
    ts(v("U"), v("ct", 0, 144), kf(1), ALU.is_equal)
    ts(v("BDn"), v("ct", 144, 272), kf(1), ALU.is_equal, -1.0, ALU.mult)
    mode[0] = 12.0
    for h in range(2):
        asel(v("CI", 128 * h, 128 * h + 128), v("ones", 0, 128), [[-1, 128]], 0, 1)
    iota(v("DL"), [[0, 3], [16, 16]], W, 0)
    iota(v("dum"), [[128, 2], [0, 8]], W, 1)
    iota(v("idp"), [[-128, 2], [-256, 8]], 2047, -1)
    iota(v("ida"), [[-128, 2], [0, 8]], 255, -1)
    iota(v("P15"), [[0, 8], [-1, 16]], 15, 0)
    ts(kf(15), kf(0), 3.0, ALU.is_equal)
    for c in range(4):
        o, i = v("SV", 192 * c, 192 * c + 192), v("SVb", 192 * c, 192 * c + 192)
        iota(i, [[-64, 8], [0, 3], [256, 8]], 960 - 2047 + 128 * (c // 2) - 512 * (c % 2), 0)
        act(i, i, AF.Identity, 0.0, kf(15))
        asel(o, i, [[0, 8], [1, 3], [16, 8]], 0, -1, ALU.not_equal, 1.0)
    ts(v("RU"), v("ct", 144, 272, 16), kf(1), ALU.is_equal)
    ts(v("RU32"), v("ct", 144, 272, 16), kf(1), ALU.is_equal, 32.0, ALU.mult)
    ts(v("RST"), v("MQ", 0, 128), 0.0, ALU.is_gt)
    ts(v("sgn"), v("MQ", 0, 16), kf(2), ALU.not_equal, 2.0, ALU.mult)
    ts(v("sgn"), v("sgn"), -1.0, ALU.add)
    ts(v("MQ"), v("MQ"), kf(2), ALU.is_equal)
    mset(ac(5), -2048.0)
    ts(ac(6), kf(2), -1.0, ALU.mult, 15.0 + 32 * 2048, ALU.add)
    ts(ac(7), kf(0), -1.0, ALU.mult)
    ts(v("acol", 8, 10), v("ida", 0, 16, 8), -1.0, ALU.mult, -12.0 * BIG, ALU.add)
    mset(ac(10), 1.0)
    mset(ac(11), -256.0)
    mset(v("G1s", 256, 264), 0.0)
    mset(v("G1s", 520, 528), 0.0)
    for r4 in range(4):
        ts(kf(16 + r4), kf(3), float(r4), ALU.is_equal)
        ts(v("SELg", 128 * r4, 128 * r4 + 128), v("MQ", 0, 128), kf(16 + r4), ALU.mult)
    ts(v("DL"), v("DL"), kf(2), ALU.add)
    ts(v("DL", 16, 32), v("DL", 16, 32), 256.0, ALU.add)
    act(v("NI"), v("CI", 0, 128), AF.Identity, 0.0, -1.0)
    if GS:
        act(v("Ib", 0, 128), v("CI", 0, 128), AF.Copy)
        act(v("Ib", 128, 256), v("NI"), AF.Copy)
    act(v("KX"), v("zer", 0, 256), AF.Copy)
    cp(v("KX", 14, 256, 16), v("ida"))
    act(s_("k1", 11), v("zer", 0, 176), AF.Copy)
    act(s_("thv"), v("zer", 0, 16), AF.Copy)
    act(s_("D1"), v("zer", 0, 16), AF.Copy)
    act(s_("B0"), v("zer", 0, 16), AF.Tanh)
    ts(v("Cw", 0, 1), kf(2), 12.0, ALU.is_lt)
    for k in range(12):
        for c in range(0, 1 << k, 512):
            n = min(512, 1 << k)
            act(v("Cw", (1 << k) + c, (1 << k) + c + n), v("Cw", c, c + n), AF.Identity, 0.0, v("sgn", k, k + 1))
    ts(v("ct", 304, 305), kf(2), 12.0, ALU.is_lt, BIG, ALU.mult)
    ts(v("ct", 305, 306), kf(2), 12.0, ALU.is_ge, 8.0, ALU.mult)
    ts(v("ct", 306, 307), kf(2), 14.0, ALU.is_ge, -7.0, ALU.mult)
    ts(v("ct", 307, 308), kf(2), 15.0, ALU.is_ge, -1.0, ALU.mult)
    ts(v("ct", 305, 306), v("ct", 305, 306), v("ct", 306, 307), ALU.add, v("ct", 307, 308), ALU.add)
    ts(v("ct", 308, 309), kf(4), -1.0, ALU.mult, 1.0, ALU.add)
    ts(v("acol", 0, 2), v("ct", 304, 306), v("ct", 308, 309), ALU.mult)
    ts(v("acol", 2, 4), v("ct", 304, 306), kf(4), ALU.mult)
    mode[0] = 30.0
    for c in range(18):
        act(v("Tw", 256 * c, 256 * c + 256), v("zer", 0, 256), AF.Copy)
    for c in range(0, W + 256, 512):
        n = min(512, W + 256 - c)
        asel(v("Vw", c, c + n), v("zer", 0, n), [[0, n]], -3, 1, ALU.not_equal, 1.0)
    mode[0] = None

    def load_f(b):
        dma("s", v("Fb%d" % b), d("LF", T.LF[RB[b]:RB[b] + 4], RB[b], RB[b] + 4), "d%d" % (6 + b),
            waits=[("fA", 6) if b == 0 else ("fB", 8)])

    def load_n(b):
        w = [("nA", 6) if b == 0 else ("nB", 8)]
        dma("s", v("Nb%d" % b), d("LN", T.LN[RB[b]:RB[b] + 4], RB[b], RB[b] + 4), "d%d" % (8 + b), waits=w)
        dma("s", v("HL", p0=16 * RB[b], p1=16 * RB[b] + 64), d("LN", T.LN[RB[b]:RB[b] + 4, 3::4, 58:66], RB[b], RB[b] + 4),
            "d%d" % (10 + b), waits=w)

    def spread(sel, src, win, b, bank0, col, ks):
        for r4 in range(4):
            bank = "ps%d" % (bank0 + r4)
            for x in range(2):
                mm(v(bank, 256 * x, 256 * x + 256), v(sel, (2 * r4 + x) * 128, (2 * r4 + x + 1) * 128), src)
            c = (RB[b] + r4) * 512
            evac(ks[r4], v(win, c, c + 512), v(bank), 1.0, col)

    def prep_n(b, ks):
        cp(v("NBf", 256 * b, 256 * b + 256), v("Nb%d" % b, 0, 256))
        ts(v("NBh", 256 * b, 256 * b + 256), v("Nb%d" % b, 0, 256), -2048.0, ALU.add)
        spread("SELh", v("NBh", 256 * b, 256 * b + 256), "NBw", b, 4, ac(4), ks)

    def gains(b, bank, other=(), banks=()):
        c = 256 * b
        yo, yi = v("Yt", c, c + 256), v("NBf", c, c + 256)
        add("v", lambda q: q.transpose(yo[0], yi[0]), [yo], [yi], 0.32)
        cp(v("OT", c, c + 256), ind(yo, co(PERM, PERM + 16)))
        m = v("Mt", c, c + 256)
        act(m, ind(v("Fw"), co(MA + 16 * b, MA + 16 * b + 16)), AF.Copy)
        gm = lambda p: v("Gm", 16 * c + 256 * p, 16 * c + 256 * p + 256)
        for p in range(16):
            src = ind(v("Fw"), v("OT", c + 16 * p, c + 16 * p + 16))
            if p in other:
                k = other.index(p) % 2
                f = v("Gf", 256 * k, 256 * k + 256)
                mode[1] = "gains2"
                act(f, src, AF.Copy)
                mode[1] = None
                mm(v(banks[k], 0, 256), v("Ib", 128, 256), m, True, False)
                mm(v(banks[k], 0, 256), v("Ib", 0, 128), f, False, True)
                act(gm(p), v(banks[k], 0, 256), AF.Relu)
            else:
                mode[0], mode[1] = D2, "gains"
                tt(gm(p), src, m, ALU.max)
                mode[0], mode[1] = None, None
        mm(v(bank, 0, 256), v("BDn"), m, True, False)
        for p in other:
            mm(v(bank, 0, 256), v("U", 15 - p, 143 - p), m, False, False)
        for p in range(16):
            mm(v(bank, 0, 256), v("U", 15 - p, 143 - p), gm(p), False, p == 15)
        act(v("G1s", 264 * b, 264 * b + 256), v(bank, 0, 256), AF.Identity, ac(5))

    def gains_spread(b, banks, ks):
        for x in range(2):
            cp(v("Gx", 512 * b + 256 * x, 512 * b + 256 * x + 256),
               ind(v("G1s", 264 * b, 264 * b + 264), co(GEXP + 16 * x, GEXP + 16 * x + 16)))
        for r4 in range(4):
            mm(v(banks[r4]), v("SELg", 128 * r4, 128 * r4 + 128), v("Gx", 512 * b, 512 * b + 512))
            c = (RB[b] + r4) * 512
            evac(ks[r4], v("Gw", c, c + 512), v(banks[r4]), 32.0, ac(6))

    load_f(0)
    load_n(0)
    load_f(1)
    load_n(1)
    mode[0] = D1
    spread("SELb", v("Fb0"), "Fw", 0, 0, None, [0, 0, 0, 0])
    prep_n(0, [1, 1, 1, 1])
    spread("SELb", v("Fb1"), "Fw", 1, 0, None, [0, 1, 0, 1])
    mode[0] = None
    prep_n(1, [1, 0, 1, 1])

    def to_list(x, n, ex, e0, bank, dummy, lst=EXP):
        if dummy is not None:
            mm(v(bank, 0, n), v("CI", 0, 128), v("DL", dummy, dummy + n), True, False)
        for c in range(0, n, 16):
            tt(v(ex, e0 + 16 * c, e0 + 16 * c + 256), ind(x, co(lst + c, lst + c + 16)), v("MQ"), ALU.mult)
        for h in range(n // 8):
            mm(v(bank, 8 * h, 8 * h + 8), v(ex, e0 + 128 * h, e0 + 128 * h + 128), v("RU"), dummy is None,
               dummy is None or h == n // 8 - 1)

    def cut(rnd):
        cp(v("CG", 0, 384), ind(v("Tw"), v("CL", 0, 24)))
        act(v("CG", 384, 768), ind(v("Tw"), v("CL", 24, 48)), AF.Copy)
        if rnd > 1:
            for c in range(2):
                act(v("CG", 768 + 384 * c, 1152 + 384 * c), ind(v("Tw"), v("CL", 48 + 24 * c, 72 + 24 * c)), AF.Copy)
        sh = [15, 127, 31]

        def back(k, bank, key, pos, out):
            mm(v(bank, 0, 48), v("CI", 0, 128), v("zer", 0, 48), True, False)
            for t in range(3):
                mm(v(bank, 16 * t, 16 * t + 16), v("NI"), key, False, False)
            for t in range(3):
                for h in range(2):
                    c = (3 * k + t) * 256 + 128 * h
                    o = 16 * pos[t] + 8 * h
                    mm(v(bank, o, o + 8), v("CG", c, c + 128), v("CI", sh[t], sh[t] + 113, 16), False, t == 2 and h == 1)
            ts(out, v(bank, 0, 48), 0.0, ALU.is_lt)
        back(0, "ps0", s_("K0"), [0, 1, 2], s_("f0a", 3))
        tt(s_("x1"), s_("f0a"), s_("f0b"), ALU.mult)
        tt(s_("x2"), s_("f0c"), s_("S0d"), ALU.mult)
        tt(s_("XL"), s_("x1"), s_("x2"), ALU.mult)
        to_list(s_("XL"), 16, "EX", 0, "ps1", 0)
        tt(s_("k0"), s_("x1"), s_("f0c"), ALU.mult)
        cp(v("lu"), v("ps1", 0, 16))
        cp(v("off"), ind(v("NBw"), v("lu")))
        if rnd > 1:
            back(1, "ps2", s_("K1"), [2, 0, 1], s_("f1b", 3))

    def after_cut(rnd):
        last = rnd == RO - 1
        if not last:
            act(s_("Lf"), v("ps1", 0, 16), AF.Copy)
            ts(s_("Lm"), s_("Lf"), float(W), ALU.is_lt, 2.0 * W, ALU.mult)
            act(s_("k0b"), s_("k0"), AF.Copy)
            act(s_("n0", 2), s_("k0", 2), AF.Identity, ac(10), -1.0)
        else:
            act(s_("n0"), s_("k0"), AF.Identity, ac(10), -1.0)
        if rnd > 1:
            tt(s_("a2"), s_("f1a"), s_("f1b"), ALU.mult)
            tt(s_("a3"), s_("f1c"), s_("k0"), ALU.mult)
            tt(s_("k1"), s_("a2"), s_("a3"), ALU.mult)
            act(s_("cb"), s_("k1"), AF.Identity, ac(10), -1.0)
            tt(s_("csa"), s_("k1"), s_("cs"), ALU.mult)
            tt(s_("n1"), s_("k0"), s_("k1"), ALU.subtract)
            tt(s_("a1", 2), s_("f1a", 2), s_("k1", 2), ALU.subtract)
            tt(s_("DR1", 2), s_("a1", 2), s_("S1d", 2), ALU.mult)
            if not last:
                act(s_("k1b"), s_("k1"), AF.Copy)
            n = 32
            to_list(s_("DR1", 2), n, "EX2", 0, "ps2", 16)
        else:
            act(s_("n1"), s_("k0"), AF.Copy)
            tt(s_("a0"), s_("f0a"), s_("k0"), ALU.subtract)
            tt(s_("DR0"), s_("a0"), s_("S0d"), ALU.mult)
            n = 16
            to_list(s_("DR0"), n, "EX2", 0, "ps2", 0)
        if not last:
            tt(s_("S0a", 3), s_("k0", 3), s_("S0d", 3), ALU.mult)
        cp(v("du", 0, n), v("ps2", 0, n))
        act(ind(v("Tw"), v("du", 0, n)), v("zer", 0, 16 * n), AF.Tanh)

    def best(h, cbank):
        c = 128 * h
        scan(v("sc1", c, c + 128), v("RST"), v("sc", c, c + 128), ALU.mult, ALU.max)
        tt(v("m4", c, c + 128), ind(v("sc1", c, c + 128), co(E15, E15 + 8)), v("sc", c, c + 128), ALU.is_equal)
        tt(v("m5", c, c + 128), v("m4", c, c + 128), v(cbank, c, c + 128), ALU.mult)
        scan(v("sc2", c, c + 128), v("RST"), v("m5", c, c + 128), ALU.mult, ALU.max)

    def choose(rnd):
        if rnd > 1:
            tt(s_("mm"), v("sc1", 15, 256, 16), s_("cb"), ALU.mult)
            mx = s_("mm")
        else:
            mx = v("sc1", 15, 256, 16)
        ts(s_("g32"), mx, 1.5 * 2 ** 28, ALU.add, 1.5 * 2 ** 28, ALU.subtract)
        ts(v("KX", 12, 256, 16), s_("g32"), 1.5 * 2 ** 36, ALU.add, 1.5 * 2 ** 36, ALU.subtract)
        act(s_("c5"), s_("g32"), AF.Identity, 0.0, 64.0)
        tt(v("KX", 13, 256, 16), s_("g32"), v("KX", 12, 256, 16), ALU.subtract)
        tt(v("KX", 15, 256, 16), s_("c5"), v("idp"), ALU.add)
        if rnd > 1:
            tt(s_("c1"), v("sc2", 15, 256, 16), s_("cb"), ALU.mult)
            tt(s_("cs"), s_("c1"), s_("csa"), ALU.add)
            to_list(s_("cs"), 16, "EX", 256, "ps1", None)
        else:
            to_list(v("sc2"), 16, "EX", 256, "ps1", None, E15)
            act(s_("cs"), v("sc2", 15, 256, 16), AF.Copy)
        for h in range(2):
            mm(v("ps0", 128 * h, 128 * h + 128), v("KX", 128 * h, 128 * h + 128), v("CI", 0, 128))
        act(v("Pv"), v("ps0", 0, 256), AF.Copy)
        act(s_("bid"), s_("g32"), AF.Sign)
        for h in range(2):
            act(sx("nthr", 8 * h, 8 * h + 8), sx("g32", 8 * h, 8 * h + 8), AF.Identity, ac(8 + h), -8.0)
            if NV[rnd]:
                act(sx("thv", 8 * h, 8 * h + 2 * NV[rnd], 2), sx("nthr", 8 * h, 8 * h + 2 * NV[rnd], 2), AF.Identity, 0.0, -1.0)
        cp(v("bu"), v("ps1", 0, 16))
        tt(v("Bt"), ind(v("Cw"), v("bu")), v("Pv"), ALU.add)
        for e in range(2):
            ts(v("At", 256 * e, 256 * e + 256), v("Bt"), ac(2 * e), ALU.mult, ac(2 * e + 1), ALU.add)
        if rnd < RO - 1:
            c = 0 if rnd == 0 else 16
            act(v("BL", c, c + 16), v("ps1", 0, 16), AF.Copy)
        tt(s_("csd"), s_("cs"), v("dum"), ALU.subtract)
        tt(s_("csb"), s_("csd"), s_("bid"), ALU.mult)

    def pairwise(rnd, banks):
        for r in range(N):
            bank = "ps%d" % banks[r % len(banks)]
            p0 = 32 * (r // 2)
            for h in range(2):
                c = 256 * (r % 2) + 128 * h
                mm(v(bank, 256 * h, 256 * h + 256), v("At", c, c + 128, None, p0, p0 + 32), v("Bt", 0, 256, None, p0, p0 + 32))
            for h in range(2):
                c = 8 * h + r
                src = v(bank, 256 * h, 256 * h + 256)
                o = sx("R", c, c + 1)
                if r % 2 == 0 and r < 2 * NV[rnd]:
                    add("v", lambda q, o=o, src=src: q.tensor_reduce(o[0], src[0], AxisListType.X, ALU.max), [o], [src], 0.32)
                else:
                    act(v("junk", 256 * c, 256 * c + 256), src, AF.Relu, sx("nthr", c, c + 1), 1.0, o)
        tt(s_("w"), s_("R"), s_("thv"), ALU.is_le)

    def state(rnd):
        act(s_("key"), v("KX", 15, 256, 16), AF.Identity, ac(10))
        if rnd == 0:
            tt(s_("K0"), s_("key"), s_("bid"), ALU.mult)
            act(s_("S0d"), s_("csd"), AF.Copy)
            return
        tt(s_("kp"), s_("key"), s_("bid"), ALU.mult)
        act(s_("kpb"), s_("kp"), AF.Copy)
        act(s_("S1d"), s_("csd"), AF.Identity, ac(11))
        tt(s_("e1", 3), s_("n0", 3), s_("csd", 3), ALU.mult)
        tt(s_("S0d", 3), s_("S0a", 3), s_("e1", 3), ALU.add)

    def slot_lists(rnd, bank):
        nk = 1 if rnd == 0 else 2
        if rnd > 0:
            tt(s_("x3"), v("BL", 16, 32), s_("Lm"), ALU.add)
            tt(v("BL", 0, 16), s_("x3"), s_("Lf"), ALU.min)
        for k in range(nk):
            for t, c in enumerate([0, 16, 112]):
                mm(v(bank, 48 * k + 16 * t, 48 * k + 16 * t + 16), v("CI", c, c + 128), v("BL", 16 * k, 16 * k + 16))
        cp(v("CL", 0, 48 * nk), v(bank, 0, 48 * nk))

    def table(rnd, bank):
        tt(s_("XW"), s_("w"), s_("csb"), ALU.mult)
        to_list(s_("XW"), 16, "EX", 512, bank, 0)
        state(rnd)
        cp(v("wu"), v(bank, 0, 16))
        cp(ind(v("Tw"), v("wu")), v("Pv"))
        dma("s", v("Vw", 0, W, None, 0, 128, 16), v("Tw", 0, W, None, 15, 128, 16), "d12", c=3.2)
        dma("s", v("Vw", 0, W, None, 17, 128, 16), v("Tw", 0, W, None, 15, 112, 16), "d13", c=3.2)
        dma("s", v("Vw", 0, W, None, 2, 112, 16), v("Tw", 0, W, None, 31, 128, 16), "d14", c=3.2)
        dma("s", v("Vw", 0, W, None, 1, 2), v("Tw", 0, W, None, 127, 128), "d15", c=3.2)
        dma("s", v("Vw", 0, W, None, 114, 115), v("Tw", 0, W, None, 15, 16), "d16", c=3.2)

    gains(0, "ps3", GS, ["ps4", "ps6"])
    cp(v("off"), ind(v("NBw", 0, W), v("HL")))
    act(v("NBw", W, W + 256), ind(v("NBw", 0, W), v("HL")), AF.Copy)
    for c in range(8):
        o, i = v("GB", 512 * c, 512 * c + 512), ind(v("Fw"), v("off", 32 * c, 32 * c + 32))
        if c in R1V:
            cp(o, i)
        else:
            act(o, i, AF.Copy)
    for h in range(2):
        mm(v("ps7", 128 * h, 128 * h + 128), v("NBw", W + 128 * h, W + 128 * h + 128), v("CI", 0, 128))
    for h in range(2):
        for p in range(16):
            mm(v("ps5", p, 128, 16), v("GB", 2048 * h + p, 2048 * h + 2048, 16), v("RU32"))
        tt(v("sc", 128 * h, 128 * h + 128), v("ps5", 0, 128), v("P15"), ALU.add)
        best(h, "ps7")
    for h in range(2):
        mm(v("ps5", 128 * h, 128 * h + 128), v("sc", 128 * h, 128 * h + 128), v("CI", 0, 128))
    act(v("Gw", W, W + 256), v("ps5", 0, 256), AF.Copy)
    choose(0)
    gains(1, "ps2")
    pairwise(0, [4, 5, 6, 7])
    slot_lists(0, "ps1")
    table(0, "ps0")
    gains_spread(0, ["ps3", "ps5", "ps7", "ps3"], [1, 1, 1, 1])
    gains_spread(1, ["ps4", "ps6", "ps2", "ps5"], [1, 0, 1, 0])

    for rnd in range(1, RO):
        last = rnd == RO - 1
        cut(rnd)
        act(v("grow"), ind(v("Gw"), v("lu")), AF.Copy)
        act(v("crow"), ind(v("NBw"), v("lu")), AF.Copy)
        for c in range(8):
            o, i = v("GV", 512 * c, 512 * c + 512), ind(v("Vw", 0, W), v("off", 32 * c, 32 * c + 32))
            if c in RVV:
                cp(o, i)
            else:
                act(o, i, AF.Copy)
        for h in range(2):
            c = 128 * h
            mm(v("ps6", c, c + 128), v("grow", c, c + 128), v("CI", 0, 128))
        act(v("KEY"), v("ps6", 0, 256), AF.Identity, ac(7), 64.0)
        for h in range(2):
            c = 128 * h
            mm(v("ps7", c, c + 128), v("crow", c, c + 128), v("CI", 0, 128))
        mode[1] = "turn"
        for h in range(2):
            for p in range(16):
                c = 384 * h + 24 * p
                mm(v("ps%d" % (3 + h), p, 384, 16), v("GV", 2048 * h + p, 2048 * h + 2048, 16), v("SV", c, c + 24))
        mode[1] = None
        after_cut(rnd)
        if last:
            dma("s", d("dT", T.dT[:]), v("Tw", 0, W, None, 15, 128, 16), "d17")
            dma("s", d("LT", T.LT[me], me, me + 1), v("Tw", 0, W, None, 16 * me + 15, 16 * me + 16), "d18")
            send(lambda r: T.dT[r], T.LT[me], lambda r: "tab", [d("dT", None)])
            dma("s", v("Vw", 0, W, None, 15, 128, 16), d("LT", T.LT[:]), "d19", waits=[("tab", 14)])
        for h in range(2):
            c = 128 * h
            bank = "ps%d" % (3 + h)
            act(v("m0", c, c + 128), v(bank, 0, 128), AF.Copy)
            tt(v("m1", c, c + 128), v(bank, 128, 256), v("m0", c, c + 128), ALU.max)
            tt(v("m2", c, c + 128), v(bank, 256, 384), v("m1", c, c + 128), ALU.max)
            tt(v("m3", c, c + 128), v("m2", c, c + 128), v("KEY", c, c + 128), ALU.is_lt)
            tt(v("sc", c, c + 128), v("m3", c, c + 128), v("ps6", c, c + 128), ALU.mult)
            best(h, "ps7")
        choose(rnd)
        if not last:
            pairwise(rnd, [2, 3, 4, 5, 6, 7, 0, 1])
            slot_lists(rnd, "ps3")
            table(rnd, "ps2")

    act(s_("D0"), s_("csb"), AF.Copy)
    act(s_("B1"), v("KX", 15, 256, 16), AF.Copy)
    act(s_("y1"), s_("cs"), AF.Identity, ac(10))
    tt(s_("y2"), s_("S0d"), v("dum"), ALU.add)
    tt(s_("y1"), s_("y1"), s_("bid"), ALU.mult)
    tt(s_("B3"), s_("csa"), s_("cb"), ALU.subtract)
    tt(s_("D2"), s_("y1"), s_("n0"), ALU.mult)
    tt(s_("D3"), s_("y1"), s_("n1"), ALU.mult)
    tt(s_("y2"), s_("y2"), s_("k0"), ALU.mult)
    tt(s_("B2"), s_("y2"), s_("n0"), ALU.subtract)
    cp(s_("Dm0", 4), ind(s_("D0", 4), co(MP, MP + 4)))
    cp(s_("Bm0", 4), ind(s_("B0", 4), co(MP, MP + 4)))
    pairwise(RO - 1, [2, 3, 4, 5, 6, 7, 0, 1])
    tt(s_("mt0", 4), ind(s_("w"), co(MW, MW + 4)), s_("Dm0", 4), ALU.mult)
    tt(v("msg"), s_("mt0", 4), s_("Bm0", 4), ALU.add)
    send(lambda r: T.msg[:, 8 * r:8 * r + 8], T.rcv[:, 8 * me:8 * me + 8], lambda r: "fin", [v("msg")])
    cp(v("rcv", 8 * me, 8 * me + 8), v("msg", 8 * me, 8 * me + 8))
    fin = [("fin", 14)]
    mm(v("ps2", 0, 16), v("CI", 0, 128), v("DL", 0, 16), True, False)
    cp(v("KX", 15, 128, 16), v("rcv", 2, 64, 8), fin)
    cp(v("KX", 143, 256, 16), v("rcv", 3, 64, 8), fin)
    xo, xi = v("EX", 0, 256), ind(v("rcv"), co(RX, RX + 16))
    add("v", lambda q: q.tensor_tensor(xo[0], xi[0], T.MQ[:, :], ALU.mult), [xo], [xi, v("MQ")], 0.45, waits=fin)
    for h in range(2):
        mm(v("ps4", 128 * h, 128 * h + 128), v("KX", 128 * h, 128 * h + 128), v("CI", 0, 128))
    act(v("Pv"), v("ps4", 0, 256), AF.Copy)
    for h in range(2):
        mm(v("ps2", 8 * h, 8 * h + 8), v("EX", 128 * h, 128 * h + 128), v("RU"), False, h == 1)
    cp(v("wu"), v("ps2", 0, 16))
    cp(ind(v("Vw"), v("wu")), v("Pv"))
    dma("s", d("yt", T.yt[:, :]), v("Vw", 0, W, None, 15, 128, 16), "d20")
    for c in range(4):
        mm(v("ps3", 128 * c, 128 * c + 128, None, 0, 8), v("rcv", 4 + c, 64, 8), v("CI", 0, 128), waits=fin)
    act(v("ybs"), v("ps3", 0, 512, None, 0, 8), AF.Copy)
    dma("a", d("yb", T.yb[:, :]), v("ybs"), "d21")

    emit(ops, Q, T, [("sent", sent[0])])


ORDER = {}


def arrange(ops, pred, queues):
    n = len(ops)
    succ = [[] for _ in ops]
    for i in range(n):
        for j in pred[i]:
            succ[j].append(i)
    hold = [o["c"] if o["dsem"] in (None, "remote") else 0.1 for o in ops]
    eng = [o["e"] for o in ops]
    edge = [[(j, max(lat, hold[j] if lat == 0.0 else 0.0)) for j, lat in pred[i].items()] for i in range(n)]

    def plan(bonus):
        total = 0.0
        for again in range(2):
            tail = [o["c"] + (max(0.0, total - o["due"]) if o["due"] is not None else 0.0) for o in ops]
            for i in range(n - 1, -1, -1):
                tail[i] += bonus[i]
                for j, lat in edge[i]:
                    if lat + tail[i] > tail[j]:
                        tail[j] = lat + tail[i]
            total = max(tail)
        left = [len(p) for p in pred]
        ready = {e: {} for e in queues}
        for i in range(n):
            if left[i] == 0:
                ready[eng[i]][i] = 0.0
        free = {e: 0.0 for e in queues}
        start = [0.0] * n
        order = []
        pick = {}
        end = 0.0
        while len(order) < n:
            for e in queues:
                if e in pick or not ready[e]:
                    continue
                fe = free[e]
                c = [(t if t > fe else fe, i) for i, t in ready[e].items()]
                b = max(c, key=lambda x: (tail[x[1]] - x[0], -x[1]))
                f = [x for x in c if x[0] + hold[x[1]] <= b[0] + 0.03]
                if f:
                    b = max(f, key=lambda x: (tail[x[1]] - x[0], -x[1]))
                pick[e] = b
            t, i = min(pick.values())
            del pick[eng[i]]
            del ready[eng[i]][i]
            start[i] = t
            order.append(i)
            free[eng[i]] = t + hold[i]
            end = max(end, t + ops[i]["c"])
            for k in succ[i]:
                left[k] -= 1
                if left[k] == 0:
                    ready[eng[k]][k] = max(start[j] + lat for j, lat in pred[k].items())
                    pick.pop(eng[k], None)
        return end, order, start
    rng = np.random.RandomState(SEED)
    bonus = [0.0] * n
    end, order, start = plan(bonus)
    top, keep = end, order
    for k in range(TRIES):
        before = {}
        lastq = {}
        for i in order:
            before[i] = lastq.get(eng[i])
            lastq[eng[i]] = i
        i = max(range(n), key=lambda x: start[x] + ops[x]["c"])
        pairs = []
        while True:
            j, t = None, 0.0
            for p, lat in pred[i].items():
                if start[p] + lat >= t:
                    j, t = p, start[p] + lat
            q = before[i]
            if q is not None and start[q] + hold[q] > t + 1e-6:
                x = q
                while x is not None and start[x] + hold[x] > t - 0.3:
                    pairs.append((i, x))
                    x = before[x]
                j = q
            if j is None:
                break
            i = j
        if not pairs:
            break
        b2 = list(bonus)
        for again in range(1 + int(rng.randint(2))):
            i, x = pairs[int(rng.randint(len(pairs)))]
            step = float(rng.uniform(0.1, 3.0))
            if rng.randint(2):
                b2[i] += step
            else:
                b2[x] -= step
        e2, o2, s2 = plan(b2)
        if e2 <= end + TEMP * (1.0 - k / TRIES) * float(rng.uniform()):
            end, order, start, bonus = e2, o2, s2, b2
            if end < top:
                top, keep = end, order
    return keep


def emit(ops, Q, T, extra):
    n = len(ops)
    hist = {}
    hard = []
    soft = []
    feeder = {}
    for i, o in enumerate(ops):
        dp = set()
        so = set()
        mine = o["dsem"] is None
        for reg, wr in [(r, False) for r in o["r"]] + [(r, True) for r in o["w"]]:
            psum = reg[0][:2] == "ps"
            for j, r2, w2 in hist.get(reg[0], []):
                if not (reg[1] & r2[1] and reg[2] & r2[2]):
                    continue
                if ops[j]["dsem"] == "remote":
                    if wr:
                        so.add(j)
                elif mine and ops[j]["dsem"] is None and ops[j]["e"] == o["e"]:
                    if o["e"] == "t":
                        if wr:
                            so.add(j)
                    elif wr or w2:
                        dp.add(j)
                elif wr or w2 or psum:
                    dp.add(j)
        for reg in o["r"]:
            hist.setdefault(reg[0], []).append((i, reg, False))
        for reg in o["w"]:
            hist.setdefault(reg[0], []).append((i, reg, True))
        if o["chain"] is not None:
            if o["chain"] in feeder:
                so.add(feeder[o["chain"]])
            feeder[o["chain"]] = i
        for s in o["feeds"]:
            feeder[s] = i
        hard.append(dp)
        soft.append(so - dp)
    pred = []
    for i, o in enumerate(ops):
        p = {j: ops[j]["c"] + WAKE for j in hard[i]}
        for j in soft[i]:
            p[j] = 0.0
        for s, _ in o["waits"]:
            p[feeder[s]] = ARRIVE[s]
        pred.append(p)
    if n not in ORDER:
        ORDER[n] = arrange(ops, pred, list(Q))
    order = ORDER[n]
    place = {i: k for k, i in enumerate(order)}
    deps = {}
    need = set()
    for i in order:
        latest = {}
        keep = []
        for j in hard[i]:
            if ops[j]["dsem"] is None:
                e = ops[j]["e"]
                if e not in latest or place[j] > place[latest[e]]:
                    latest[e] = j
            else:
                keep.append(j)
        deps[i] = keep + list(latest.values())
        need.update(deps[i])
    count = {}
    val = {}
    seen = {}
    for i in order:
        o = ops[i]
        q = Q[o["e"]]
        want = {}
        for s, k in o["waits"]:
            want[s] = max(want.get(s, 0), k)
        for j in deps[i]:
            s, k = val[j]
            want[s] = max(want.get(s, 0), k)
        for s in sorted(want):
            if seen.get((o["e"], s), 0) < want[s]:
                q.wait_ge(T.sem[s], want[s])
                seen[(o["e"], s)] = want[s]
        ins = o["fn"](q)
        if o["dsem"] == "remote":
            continue
        if o["dsem"] is not None:
            s, k = o["dsem"], 16
        elif i in need:
            s, k = "c" + o["e"], 1
        else:
            continue
        ins.then_inc(T.sem[s], k)
        count[s] = count.get(s, 0) + k
        val[i] = (s, count[s])
    for s, k in sorted(count.items()) + extra:
        if max([0] + [x for (e, s2), x in seen.items() if s2 == s]) < k:
            Q["g"].wait_ge(T.sem[s], k)
